import numpy as np
import ml_dtypes


def mxq(x, axis, fmt="e4m3"):
    dtype, down = {"e4m3": (ml_dtypes.float8_e4m3fn, 7), "e5m2": (ml_dtypes.float8_e5m2, 14)}[fmt]
    v = np.moveaxis(np.asarray(x, np.float32).astype(ml_dtypes.bfloat16).astype(np.float64), axis, -1)
    blocks = v.reshape(v.shape[:-1] + (-1, 32))
    amax = np.abs(blocks).max(-1, keepdims=True)
    byte = np.maximum(np.where(amax > 0, np.frexp(amax)[1] - 1 + 127, 0) - down, 1)
    scale = np.exp2(byte - 127.0)
    codes = (blocks / scale).astype(np.float32).astype(dtype).astype(np.float64)
    return np.moveaxis((codes * scale).reshape(v.shape), -1, axis)


WIDE = False


def mx_kscale(k):
    if not WIDE:
        return np.ones(k)
    levels = np.array([10, -10, 5, -5, 0])
    if k % 512:
        return np.exp2(np.random.permutation(np.resize(levels, k // 32))).repeat(32)
    a = np.empty((k // 512, 16))
    for p in range(k // 512):
        a[p, :8] = np.random.permutation(np.resize(levels, 8))
        for g in range(8):
            far = levels[np.abs(levels - a[p, g]) >= 10]
            a[p, g + 8] = far[np.random.randint(len(far))]
    return np.exp2(a.ravel()).repeat(32)


BF16 = ml_dtypes.bfloat16


def bf(x):
    return np.asarray(x, np.float32).astype(BF16)


def f64(x):
    return np.asarray(x).astype(np.float64)


E2M1 = np.array([0.0, 0.5, 1.0, 1.5, 2.0, 3.0, 4.0, 6.0, -0.0, -0.5, -1.0, -1.5, -2.0, -3.0, -4.0, -6.0])


def pack_weight(w, fmt):
    k, n = w.shape
    w = f64(bf(w)).reshape(k // 32, 32, n)
    amax = np.abs(w).max(1)
    if fmt == "e4m3":
        byte = np.frexp(amax)[1] - 1 + 127 - 7
    else:
        mant, ex = np.frexp(amax / 6.0)
        byte = np.where(mant > 0.5, ex, ex - 1) + 127
    byte = np.clip(np.where(amax > 0, byte, 1), 1, 254)
    scaled = (w * np.exp2(127.0 - byte)[:, None, :]).reshape(k, n).astype(np.float32)
    by_word = np.ascontiguousarray(scaled.reshape(k // 512, 128, 4, n).transpose(0, 1, 3, 2))
    if fmt == "e4m3":
        words = by_word.astype(ml_dtypes.float8_e4m3fn).view(np.uint8)
    else:
        c = by_word.astype(ml_dtypes.float4_e2m1fn).view(np.uint8) & 0xF
        words = c[..., 0::2] | (c[..., 1::2] << 4)
    return np.ascontiguousarray(words), np.ascontiguousarray(byte.astype(np.uint8).reshape(k // 512, 16, n))


def unpack_weight(words, scales, fmt):
    g, p, n, _ = words.shape
    if fmt == "e4m3":
        vals = np.ascontiguousarray(words).view(ml_dtypes.float8_e4m3fn).astype(np.float64)
    else:
        nib = np.empty((g, p, n, 4), np.uint8)
        nib[..., 0::2] = words & 0xF
        nib[..., 1::2] = words >> 4
        vals = E2M1[nib]
    vals = vals * np.repeat(np.exp2(scales.astype(np.float64) - 127.0), 8, axis=1)[..., None]
    return vals.transpose(0, 1, 3, 2).reshape(g * 512, n)
def pack4(w):
    words, scales = pack_weight(w, "e2m1")
    return words.reshape(words.shape[0], 128, -1), scales


def unpack4(words, scales):
    return unpack_weight(words.reshape(words.shape[0], 128, -1, 2), scales, "e2m1")


def planes(Y):
    n, m = Y.shape
    b = f64(bf(Y)).reshape(n // 32, 32, m)
    amax = np.abs(b).max(1)
    byte = np.clip(np.where(amax > 0, np.frexp(amax)[1] - 1 + 127 - 7, 1), 1, 254)
    codes = (b * np.exp2(127.0 - byte)[:, None, :]).reshape(n, m).astype(np.float32).astype(ml_dtypes.float8_e4m3fn).view(np.uint8)
    words = codes.reshape(n // 512, 128, 4, m).transpose(0, 1, 3, 2)
    return np.ascontiguousarray(words), np.ascontiguousarray(byte.astype(np.uint8).reshape(n // 512, 16, m))


G, R, D, J, P = 4, 1024, 512, 1024, 32
SD = 0.7
SHARP = 8.0

def setup_inputs():
    n = np.random.randn
    centre = SD * n(G, P, D)
    x = np.tile(centre, (1, R // P, 1)) + SD * np.exp(0.3 * n(G, R, 1)) * n(G, R, D)
    c = np.tile(centre, (1, J // P, 1)) + SD * n(G, J, D)
    prec = SHARP * D ** -0.5 * np.exp(0.3 * n(G, D))
    rho = np.exp(0.3 * n(G, J))
    bias = n(G, J) - 2.0 - 0.5 * D ** -0.5 * (c * c * prec[:, None, :]).sum(-1)
    s = np.stack([mx_kscale(D) for _ in range(G)])
    t = np.stack([mx_kscale(J) for _ in range(G)])
    b_words, b_scales = pack4((c.transpose(0, 2, 1) * D ** -0.5 * s[:, :, None]).reshape(G * D, J))
    h_words, h_scales = pack4((c / (rho * t)[:, :, None]).reshape(G * J, D))
    return {"x": bf(x), "prec": bf(prec / s), "b_words": b_words, "b_scales": b_scales, "bias": bf(bias),
            "rho": bf(rho * t), "h_words": h_words, "h_scales": h_scales, "metric": bf(np.exp(0.8 * n(G, D)))}

def reference(x, prec, b_words, b_scales, bias, rho, h_words, h_scales, metric):
    x = f64(x)
    b = unpack4(b_words, b_scales).reshape(G, D, J)
    h = unpack4(h_words, h_scales).reshape(G, J, D)
    xp = x * f64(prec)[:, None, :]
    aff = np.exp((mxq(xp, 2) @ b) + f64(bias)[:, None, :])
    total = aff.sum(axis=2, keepdims=True)
    ar = aff * f64(rho)[:, None, :]
    mean = (mxq(ar, 2) @ h) / total
    y = np.square(mean - x) * f64(metric)[:, None, :]
    Y = y.transpose(2, 0, 1).reshape(D, G * R)
    words, scales = planes(Y)
    return y, words, scales

@@ -1,0 +1,321 @@
+from contextlib import ExitStack
+
+import concourse.mybir as mybir
+from concourse.masks import make_identity
+
+G, R, D, J = 4, 1024, 512, 1024
+FLOPS = 2 * 2 * G * R * D * J
+
+F32 = mybir.dt.float32
+BF16 = mybir.dt.bfloat16
+I32 = mybir.dt.int32
+U32 = mybir.dt.uint32
+U8 = mybir.dt.uint8
+FP8X4 = mybir.dt.float8_e4m3fn_x4
+FP4X4 = mybir.dt.float4_e2m1fn_x4
+ALU = mybir.AluOpType
+ACT = mybir.ActivationFunctionType
+
+P = 128
+STEP = 512
+STEPS = G * R // STEP
+TILES = STEP // P
+RING = 7
+RHO_COL = 384
+
+ORDER = "H I X S M Ex Qy Ex E M F M S X D E S S Ex F E Ex B M F E B G Ex F G T T D H B B Qa Y Qa G H W T W T J S W J S Y J S G J R S Qx I Ex H Ex Ex".split()
+COUNT = {"X": 2, "D": 2, "Qx": 1, "S": 8, "Ex": 8, "B": 4, "Qa": 2, "T": 4, "J": 4, "R": 1, "M": 4,
+         "E": 4, "F": 4, "G": 4, "H": 4, "Y": 2, "I": 2, "Qy": 1, "W": 3}
+PHASE = {"X":4,"D":4,"Qx":2,"S":6,"Ex":5,"B":0,"Qa":0,"T":0,"J":0,"R":0,"M":-4,"E":-4,"F":-4,"G":-4,"H":-5,"Y":-3,"I":-4,"Qy":-3,"W":4}
+CAST_ON = ["ACT","ACT","POOL","POOL"]
+TOT_PER_BANK = 4
+LEAD = 4
+
+
+def tile_mean_shift_displacement_k7_kernel(
+    tc, x, prec, b_words, b_scales, bias, rho, h_words, h_scales, metric, out_0, out_1, out_2
+):
+    nc = tc.nc
+    with ExitStack() as ctx:
+        keep = ctx.enter_context(tc.tile_pool(name="keep", bufs=1))
+        psum = ctx.enter_context(tc.psum_pool(name="psum", bufs=1))
+
+        def sb(name, shape, dtype):
+            return keep.tile(shape, dtype, name=name, align_bytes=64)
+
+        def sbs(name, n, shape, dtype):
+            return [sb("%s%d" % (name, k), shape, dtype) for k in range(n)]
+
+        banks = [psum.tile([P, 512], F32, name="bank%d" % k) for k in range(RING)]
+        rho_bank = psum.tile([P, 512], F32, name="rho_bank")
+
+        ident = sb("ident", [P, P], F32)
+        ident_bf = sb("ident_bf", [P, P], BF16)
+        warm = sb("warm", [P, 1], F32)
+        prec_sb = sb("prec_sb", [P, G, 4], BF16)
+        bias_sb = sb("bias_sb", [P, G * 2, 4], BF16)
+        rho_sb = sb("rho_sb", [P, G * 2, 4], BF16)
+        metric_sb = sbs("metric_sb", G, [P, D], BF16)
+        x_sb = sbs("x_sb", STEPS, [P, TILES, D], BF16)
+        b_raw = sbs("b_raw", G, [P, 2 * J], U8)
+        bs_raw = sb("bs_raw", [P, G, J], U8)
+        b_perm = sbs("b_perm", G, [P, 2 * J], U8)
+        bs_perm = sbs("bs_perm", G, [P, J], U8)
+        h_sb = sbs("h_sb", G, [P, 2, 2 * D], U8)
+        hs_sb = sb("hs_sb", [P, 2 * G, D], U8)
+        xp = sbs("xp", 2, [P, STEP, 4], BF16)
+        xq = sbs("xq", 2, [P, STEP], U32)
+        xs = sbs("xs", 2, [P, STEP], U8)
+        aff = sbs("aff", 2, [P, 8, STEP], F32)
+        ar = sbs("ar", 2, [P, 2, STEP, 4], BF16)
+        arq = sbs("arq", 2, [P, 2, STEP], U32)
+        ars = sbs("ars", 2, [P, 2, STEP], U8)
+        spill = sb("spill", [P, TILES, P], BF16)
+        total = sbs("total", 2, [P, TILES], F32)
+        rinv = sbs("rinv", 2, [P, TILES], F32)
+        disp = sbs("disp", 2, [P, TILES, D], F32)
+        sq = sbs("sq", 2, [P, TILES, D], F32)
+        y = sbs("y", 3, [P, TILES, D], F32)
+        yb = sbs("yb", 2, [P, TILES, D], BF16)
+        yt = sbs("yt", 2, [P, STEP, 4], BF16)
+        yq = sbs("yq", 2, [P, STEP], U32)
+        ys = sb("ys", [P, G * R], U8)
+
+        ctx.enter_context(tc.manual_schedule())
+
+        def load_x(s, t0, t1):
+            a, r0 = s // 2, (s % 2) * STEP
+            nc.sync.dma_start(
+                out=x_sb[s][:, t0:t1, :],
+                in_=x[a, r0 + t0 * P : r0 + t1 * P, :].rearrange("(t p) f -> p t f", p=P),
+            )
+
+        def load_b(a):
+            nc.sync.dma_start(out=b_raw[a][:].bitcast(I32), in_=b_words[a].bitcast(I32))
+
+        def load_h(a):
+            nc.sync.dma_start(
+                out=h_sb[a][:].bitcast(I32),
+                in_=h_words[2 * a : 2 * a + 2].rearrange("g p n -> p g n").bitcast(I32),
+            )
+
+        def load_scales(dst, src):
+            for q in range(4):
+                nc.sync.dma_start(
+                    out=dst[32 * q : 32 * q + 4, :, :].bitcast(I32),
+                    in_=src[:, 4 * q : 4 * q + 4, :].rearrange("g r n -> r g n").bitcast(I32),
+                )
+
+        def load_metric(a):
+            nc.sync.dma_start(out=metric_sb[a][:], in_=metric[a].partition_broadcast(P))
+
+        nc.vector.memset(bs_raw[:].bitcast(I32), 0)
+        nc.vector.memset(hs_sb[:].bitcast(I32), 0)
+        make_identity(nc, ident[:])
+        make_identity(nc, ident_bf[:])
+        nc.scalar.dma_start(out=prec_sb[:], in_=prec.rearrange("a (p t) -> p a t", t=4))
+        nc.scalar.dma_start(out=bias_sb[:], in_=bias.rearrange("a (g p t) -> p (a g) t", p=P, t=4))
+        nc.scalar.dma_start(out=rho_sb[:], in_=rho.rearrange("a (g p t) -> p (a g) t", p=P, t=4))
+        nc.scalar.activation(out=warm[:], in_=ident[:, 0:1], func=ACT.Exp)
+        load_x(0, 0, 2)
+        load_b(0)
+        load_x(0, 2, 4)
+        load_scales(bs_raw, b_scales)
+        load_x(1, 0, TILES)
+        load_b(1)
+        load_h(0)
+        load_scales(hs_sb, h_scales)
+        load_x(2, 0, TILES)
+        load_metric(0)
+        load_b(2)
+        load_b(3)
+        for s in range(3, STEPS):
+            load_x(s, 0, TILES)
+            if s % 2 == 1 and s // 2 < G:
+                load_h(s // 2)
+                load_metric(s // 2)
+
+        def permute(a, piece):
+            if piece < 2:
+                cols = slice(piece * J, (piece + 1) * J)
+                nc.vector.tensor_copy(
+                    out=b_perm[a][:, cols].rearrange("p (t m b) -> p t m b", t=4, b=2),
+                    in_=b_raw[a][:, cols].rearrange("p (m t b) -> p t m b", t=4, b=2),
+                )
+            else:
+                nc.vector.tensor_copy(
+                    out=bs_perm[a][:].rearrange("p (g t m) -> p g t m", g=2, t=4),
+                    in_=bs_raw[:, a, :].rearrange("p (g m t) -> p g t m", g=2, t=4),
+                )
+
+        for piece in range(3):
+            permute(0, piece)
+
+        held = {}
+
+        def take_bank(key):
+            held[key] = banks[len(held) % RING]
+            return held[key]
+
+        def turn_words(bank, words, first, step, half):
+            for k in range(2):
+                for u in range(2):
+                    lo = (2 * half + k) * 256 + u * first
+                    nc.tensor.transpose(
+                        bank[:, u * 256 + k * P : u * 256 + (k + 1) * P],
+                        words[:, lo : lo + step * (P - 1) + 1 : step],
+                        ident[:],
+                    )
+
+        def emit(kind, s, i):
+            a, r0, b = s // 2, (s % 2) * STEP, s % 2
+            if kind == "W":
+                if s + 1 < G:
+                    permute(s + 1, i)
+            elif kind == "X":
+                words = x_sb[s][:].rearrange("p t f -> p (t f)").bitcast(F32)
+                turn_words(take_bank(("X", s, i)), words, 1, 2, i)
+                if s == 0 and i == 1:
+                    nc.tensor.matmul(
+                        rho_bank[:, RHO_COL : RHO_COL + 8 * G],
+                        lhsT=ident_bf[:],
+                        rhs=rho_sb[:].rearrange("p g t -> p (g t)"),
+                        start=True,
+                        stop=True,
+                    )
+            elif kind == "D":
+                nc.vector.tensor_tensor(
+                    out=xp[b][:, i * 256 : (i + 1) * 256, :].rearrange("p n (u e) -> p n u e", u=2),
+                    in0=held["X", s, i][:].bitcast(BF16).rearrange("p (u n e) -> p n u e", u=2, e=2),
+                    in1=prec_sb[:, a, :].rearrange("p (u e) -> p u e", u=2).unsqueeze(1).to_broadcast([P, 256, 2, 2]),
+                    op=ALU.mult,
+                )
+            elif kind == "Qx":
+                nc.vector.quantize_mx(
+                    out=xq[b][:].bitcast(FP8X4), scales=xs[b][:], in_=xp[b][:].rearrange("p n t -> p (n t)")
+                )
+            elif kind == "S":
+                nc.tensor.matmul_mx(
+                    out=take_bank(("S", s, i))[:],
+                    lhsT=b_perm[a][:, i * 256 : (i + 1) * 256].bitcast(FP4X4),
+                    lhsT_scale=bs_perm[a][:, i * P : (i + 1) * P],
+                    rhs=xq[b][:].bitcast(FP8X4),
+                    rhs_scale=xs[b][:],
+                    start=True,
+                    stop=True,
+                )
+            elif kind == "Ex":
+                nc.scalar.activation(
+                    out=aff[b][:, i, :],
+                    in_=held["S", s, i][:],
+                    func=ACT.Exp,
+                    bias=bias_sb[:, 2 * a + i // 4, i % 4 : i % 4 + 1],
+                )
+            elif kind == "B":
+                g, n0 = i // 2, (i % 2) * 256
+                col = RHO_COL + (2 * a + g) * 4
+                nc.vector.tensor_tensor(
+                    out=ar[b][:, g, n0 : n0 + 256, :].rearrange("p (c n) t -> p c t n", n=4),
+                    in0=aff[b][:, 4 * g : 4 * g + 4, n0 : n0 + 256].rearrange("p t (c n) -> p c t n", n=4),
+                    in1=rho_bank[:, col : col + 4].unsqueeze(1).unsqueeze(3).to_broadcast([P, 64, 4, 4]),
+                    op=ALU.mult,
+                )
+            elif kind == "Qa":
+                nc.vector.quantize_mx(
+                    out=arq[b][:, i, :].bitcast(FP8X4),
+                    scales=ars[b][:, i, :],
+                    in_=ar[b][:, i, :, :].rearrange("p n t -> p (n t)"),
+                )
+            elif kind == "T":
+                if i % TOT_PER_BANK == 0:
+                    take_bank(("T", s, i))
+                q = i % TOT_PER_BANK
+                for jt in range(8):
+                    nc.tensor.matmul(
+                        held["T", s, i - q][:, q * P : (q + 1) * P],
+                        lhsT=aff[b][:, jt, i * P : (i + 1) * P],
+                        rhs=ident[:],
+                        start=jt == 0,
+                        stop=jt == 7,
+                        is_transpose=True,
+                    )
+            elif kind == "J":
+                q = i % TOT_PER_BANK
+                nc.scalar.activation(
+                    out=spill[:, i, :],
+                    in_=held["T", s, i - q][:, q * P : (q + 1) * P],
+                    func=ACT.Copy,
+                    accum_out=total[b][:, i : i + 1],
+                )
+            elif kind == "R":
+                nc.vector.reciprocal(rinv[b][:], total[b][:])
+            elif kind == "M":
+                bank = take_bank(("M", s, i))
+                for g in range(2):
+                    nc.tensor.matmul_mx(
+                        out=bank[:],
+                        lhsT=arq[b][:, g, i * P : (i + 1) * P].bitcast(FP8X4),
+                        lhsT_scale=ars[b][:, g, i * P : (i + 1) * P],
+                        rhs=h_sb[a][:, g, :].bitcast(FP4X4),
+                        rhs_scale=hs_sb[:, 2 * a + g, :],
+                        start=g == 0,
+                        stop=g == 1,
+                    )
+            elif kind == "E":
+                nc.vector.scalar_tensor_tensor(
+                    out=disp[b][:, i, :],
+                    in0=held["M", s, i][:],
+                    scalar=rinv[b][:, i : i + 1],
+                    in1=x_sb[s][:, i, :],
+                    op0=ALU.mult,
+                    op1=ALU.subtract,
+                )
+            elif kind == "F":
+                nc.scalar.activation(out=sq[b][:, i, :], in_=disp[b][:, i, :], func=ACT.Square)
+            elif kind == "G":
+                eng = nc.vector if s == STEPS - 1 else nc.gpsimd
+                eng.tensor_tensor(out=y[s % 3][:, i, :], in0=sq[b][:, i, :], in1=metric_sb[a][:], op=ALU.mult)
+                nc.sync.dma_start(out=out_0[a, r0 + i * P : r0 + (i + 1) * P, :], in_=y[s % 3][:, i, :])
+            elif kind == "H":
+                dst = yb[b][:, i, :].rearrange("p (u q e) -> p u q e", u=2, e=2)
+                src = y[s % 3][:, i, :].rearrange("p (q u e) -> p u q e", u=2, e=2)
+                where = CAST_ON[i] if s < STEPS - 1 else ("ACT", "DVE")[i % 2]
+                if where == "ACT":
+                    nc.scalar.copy(dst, src)
+                elif where == "DVE":
+                    nc.vector.tensor_copy(dst, src)
+                else:
+                    nc.gpsimd.tensor_scalar(dst, src, 1.0, 1.0, ALU.mult, ALU.mult)
+            elif kind == "Y":
+                words = yb[b][:].rearrange("p t f -> p (t f)").bitcast(F32)
+                turn_words(take_bank(("Y", s, i)), words, P, 1, i)
+            elif kind == "I":
+                words = yt[b][:].rearrange("p n t -> p (n t)").bitcast(F32)
+                nc.scalar.copy(
+                    words[:, i * 512 : (i + 1) * 512].rearrange("p (n u) -> p n u", u=2),
+                    held["Y", s, i][:].rearrange("p (u n) -> p n u", u=2),
+                )
+            elif kind == "Qy":
+                cols = slice(s * STEP, (s + 1) * STEP)
+                nc.vector.quantize_mx(
+                    out=yq[b][:].bitcast(FP8X4), scales=ys[:, cols], in_=yt[b][:].rearrange("p n t -> p (n t)")
+                )
+                nc.sync.dma_start(
+                    out=out_1[0, :, cols, :].rearrange("p n t -> p (n t)").bitcast(I32), in_=yq[b][:].bitcast(I32)
+                )
+                if s >= STEPS - 2:
+                    done = slice(0, (STEPS - 1) * STEP) if s == STEPS - 2 else cols
+                    for q in range(4):
+                        queue = nc.scalar if s == STEPS - 1 and q % 2 else nc.sync
+                        queue.dma_start(
+                            out=out_2[0, 4 * q : 4 * q + 4, done].bitcast(I32),
+                            in_=ys[32 * q : 32 * q + 4, done].bitcast(I32),
+                        )
+
+        seen = {kind: PHASE[kind] - LEAD * COUNT[kind] for kind in COUNT}
+        for turn in range(STEPS + 2 * LEAD + 1):
+            for kind in ORDER:
+                s, i = divmod(seen[kind], COUNT[kind])
+                seen[kind] += 1
+                if 0 <= s < STEPS:
+                    emit(kind, s, i)

@@ -21,14 +21,16 @@ STEP = 512
 STEPS = G * R // STEP
 TILES = STEP // P
 RING = 7
-RHO_COL = 384
+BIAS_ROW, RHO_ROW, PREC_ROW = 0, 8, 16
 
-ORDER = "H I X S M Ex Qy Ex E M F M S X D E S S Ex F E Ex B M F E B G Ex F G T T D H B B Qa Y Qa G H W T W T J S W J S Y J S G J R S Qx I Ex H Ex Ex".split()
+ORDER = "W M S D F X Ex S F Ex E E B G G S F B Ex D F B H B Qa G T J T Ex J Qa S Y T G T S Ex S W H I J S J Y R X M Ex M H S H Qx Ex Qy W E M E Ex I".split()
 COUNT = {"X": 2, "D": 2, "Qx": 1, "S": 8, "Ex": 8, "B": 4, "Qa": 2, "T": 4, "J": 4, "R": 1, "M": 4,
          "E": 4, "F": 4, "G": 4, "H": 4, "Y": 2, "I": 2, "Qy": 1, "W": 3}
-PHASE = {"X":4,"D":4,"Qx":2,"S":6,"Ex":5,"B":0,"Qa":0,"T":0,"J":0,"R":0,"M":-4,"E":-4,"F":-4,"G":-4,"H":-5,"Y":-3,"I":-4,"Qy":-3,"W":4}
-CAST_ON = ["ACT","ACT","POOL","POOL"]
-TOT_PER_BANK = 4
+PHASE = {"X":5,"D":4,"Qx":2,"S":7,"Ex":6,"B":0,"Qa":0,"T":0,"J":0,"R":0,"M":-1,"E":-2,"F":-4,"G":-4,"H":-4,"Y":-3,"I":-3,"Qy":-2,"W":3}
+CAST_ON = ["ACT","ACT","ACT","POOL"]
+WEIGH_ON = ["POOL","POOL","POOL","POOL"]
+WEIGH_WITH_NEXT = [0,0,0,0]
+TOT_PER_BANK = 1
 LEAD = 4
 
 
@@ -47,15 +49,16 @@ def tile_mean_shift_displacement_k7_kernel(
             return [sb("%s%d" % (name, k), shape, dtype) for k in range(n)]
 
         banks = [psum.tile([P, 512], F32, name="bank%d" % k) for k in range(RING)]
-        rho_bank = psum.tile([P, 512], F32, name="rho_bank")
+        const_bank = psum.tile([P, 4, P], BF16, name="const_bank")
 
         ident = sb("ident", [P, P], F32)
         ident_bf = sb("ident_bf", [P, P], BF16)
         warm = sb("warm", [P, 1], F32)
+        rows = sb("rows", [P, 512], BF16)
+        metric_rows = sb("metric_rows", [P, D], BF16)
         prec_sb = sb("prec_sb", [P, G, 4], BF16)
-        bias_sb = sb("bias_sb", [P, G * 2, 4], BF16)
-        rho_sb = sb("rho_sb", [P, G * 2, 4], BF16)
-        metric_sb = sbs("metric_sb", G, [P, D], BF16)
+        bias_sb = sb("bias_sb", [P, 4, 2 * G], F32)
+        metric_sb = sbs("metric_sb", G, [P, D], F32)
         x_sb = sbs("x_sb", STEPS, [P, TILES, D], BF16)
         b_raw = sbs("b_raw", G, [P, 2 * J], U8)
         bs_raw = sb("bs_raw", [P, G, J], U8)
@@ -106,17 +109,17 @@ def tile_mean_shift_displacement_k7_kernel(
                     in_=src[:, 4 * q : 4 * q + 4, :].rearrange("g r n -> r g n").bitcast(I32),
                 )
 
-        def load_metric(a):
-            nc.sync.dma_start(out=metric_sb[a][:], in_=metric[a].partition_broadcast(P))
-
+        nc.vector.memset(rows[:].bitcast(I32), 0)
+        nc.vector.memset(metric_rows[:].bitcast(I32), 0)
         nc.vector.memset(bs_raw[:].bitcast(I32), 0)
         nc.vector.memset(hs_sb[:].bitcast(I32), 0)
-        make_identity(nc, ident[:])
         make_identity(nc, ident_bf[:])
-        nc.scalar.dma_start(out=prec_sb[:], in_=prec.rearrange("a (p t) -> p a t", t=4))
-        nc.scalar.dma_start(out=bias_sb[:], in_=bias.rearrange("a (g p t) -> p (a g) t", p=P, t=4))
-        nc.scalar.dma_start(out=rho_sb[:], in_=rho.rearrange("a (g p t) -> p (a g) t", p=P, t=4))
-        nc.scalar.activation(out=warm[:], in_=ident[:, 0:1], func=ACT.Exp)
+        make_identity(nc, ident[:])
+        nc.scalar.dma_start(out=rows[PREC_ROW : PREC_ROW + G, :], in_=prec)
+        nc.scalar.dma_start(out=rows[BIAS_ROW : BIAS_ROW + 2 * G, :], in_=bias.rearrange("a (g n) -> (a g) n", g=2))
+        nc.scalar.dma_start(out=rows[RHO_ROW : RHO_ROW + 2 * G, :], in_=rho.rearrange("a (g n) -> (a g) n", g=2))
+        nc.scalar.dma_start(out=metric_rows[0:G, :], in_=metric)
+        nc.scalar.activation(out=warm[:], in_=ident_bf[:, 0:1], func=ACT.Exp)
         load_x(0, 0, 2)
         load_b(0)
         load_x(0, 2, 4)
@@ -126,14 +129,12 @@ def tile_mean_shift_displacement_k7_kernel(
         load_h(0)
         load_scales(hs_sb, h_scales)
         load_x(2, 0, TILES)
-        load_metric(0)
         load_b(2)
         load_b(3)
         for s in range(3, STEPS):
             load_x(s, 0, TILES)
-            if s % 2 == 1 and s // 2 < G:
+            if s % 2 == 1:
                 load_h(s // 2)
-                load_metric(s // 2)
 
         def permute(a, piece):
             if piece < 2:
@@ -148,8 +149,11 @@ def tile_mean_shift_displacement_k7_kernel(
                     in_=bs_raw[:, a, :].rearrange("p (g m t) -> p g t m", g=2, t=4),
                 )
 
-        for piece in range(3):
-            permute(0, piece)
+        for t in range(4):
+            nc.tensor.transpose(const_bank[:, t, :], rows[:, t : t + 4 * (P - 1) + 1 : 4], ident_bf[:])
+        nc.scalar.copy(prec_sb[:], const_bank[:, :, PREC_ROW : PREC_ROW + G].rearrange("p t a -> p a t"))
+        nc.scalar.copy(bias_sb[:], const_bank[:, :, BIAS_ROW : BIAS_ROW + 2 * G])
+        permute(0, 0)
 
         held = {}
 
@@ -176,13 +180,16 @@ def tile_mean_shift_displacement_k7_kernel(
                 words = x_sb[s][:].rearrange("p t f -> p (t f)").bitcast(F32)
                 turn_words(take_bank(("X", s, i)), words, 1, 2, i)
                 if s == 0 and i == 1:
-                    nc.tensor.matmul(
-                        rho_bank[:, RHO_COL : RHO_COL + 8 * G],
-                        lhsT=ident_bf[:],
-                        rhs=rho_sb[:].rearrange("p g t -> p (g t)"),
-                        start=True,
-                        stop=True,
-                    )
+                    for k in range(G):
+                        bank = take_bank(("metric", k))
+                        nc.tensor.matmul(
+                            bank[:],
+                            lhsT=ident_bf[:, k : k + 1].to_broadcast([P, P]),
+                            rhs=metric_rows[:],
+                            start=True,
+                            stop=True,
+                        )
+                        nc.scalar.copy(metric_sb[k][:], bank[:])
             elif kind == "D":
                 nc.vector.tensor_tensor(
                     out=xp[b][:, i * 256 : (i + 1) * 256, :].rearrange("p n (u e) -> p n u e", u=2),
@@ -190,10 +197,14 @@ def tile_mean_shift_displacement_k7_kernel(
                     in1=prec_sb[:, a, :].rearrange("p (u e) -> p u e", u=2).unsqueeze(1).to_broadcast([P, 256, 2, 2]),
                     op=ALU.mult,
                 )
+                if s == 0 and i == 1:
+                    permute(0, 2)
             elif kind == "Qx":
                 nc.vector.quantize_mx(
                     out=xq[b][:].bitcast(FP8X4), scales=xs[b][:], in_=xp[b][:].rearrange("p n t -> p (n t)")
                 )
+                if s == 0:
+                    permute(0, 1)
             elif kind == "S":
                 nc.tensor.matmul_mx(
                     out=take_bank(("S", s, i))[:],
@@ -209,15 +220,15 @@ def tile_mean_shift_displacement_k7_kernel(
                     out=aff[b][:, i, :],
                     in_=held["S", s, i][:],
                     func=ACT.Exp,
-                    bias=bias_sb[:, 2 * a + i // 4, i % 4 : i % 4 + 1],
+                    bias=bias_sb[:, i % 4, 2 * a + i // 4 : 2 * a + i // 4 + 1],
                 )
             elif kind == "B":
                 g, n0 = i // 2, (i % 2) * 256
-                col = RHO_COL + (2 * a + g) * 4
+                col = RHO_ROW + 2 * a + g
                 nc.vector.tensor_tensor(
-                    out=ar[b][:, g, n0 : n0 + 256, :].rearrange("p (c n) t -> p c t n", n=4),
-                    in0=aff[b][:, 4 * g : 4 * g + 4, n0 : n0 + 256].rearrange("p t (c n) -> p c t n", n=4),
-                    in1=rho_bank[:, col : col + 4].unsqueeze(1).unsqueeze(3).to_broadcast([P, 64, 4, 4]),
+                    out=ar[b][:, g, n0 : n0 + 256, :].rearrange("p (c n) t -> p c t n", n=2),
+                    in0=aff[b][:, 4 * g : 4 * g + 4, n0 : n0 + 256].rearrange("p t (c n) -> p c t n", n=2),
+                    in1=const_bank[:, :, col : col + 1].unsqueeze(1).to_broadcast([P, 128, 4, 2]),
                     op=ALU.mult,
                 )
             elif kind == "Qa":
@@ -273,9 +284,23 @@ def tile_mean_shift_displacement_k7_kernel(
             elif kind == "F":
                 nc.scalar.activation(out=sq[b][:, i, :], in_=disp[b][:, i, :], func=ACT.Square)
             elif kind == "G":
-                eng = nc.vector if s == STEPS - 1 else nc.gpsimd
-                eng.tensor_tensor(out=y[s % 3][:, i, :], in0=sq[b][:, i, :], in1=metric_sb[a][:], op=ALU.mult)
-                nc.sync.dma_start(out=out_0[a, r0 + i * P : r0 + (i + 1) * P, :], in_=y[s % 3][:, i, :])
+                last = s == STEPS - 1
+                if WEIGH_WITH_NEXT[i] and not last:
+                    return
+                j = i
+                while j > 0 and WEIGH_WITH_NEXT[j - 1] and not last:
+                    j -= 1
+                eng = nc.vector if last or WEIGH_ON[i] == "DVE" else nc.gpsimd
+                eng.tensor_tensor(
+                    out=y[s % 3][:, j : i + 1, :],
+                    in0=sq[b][:, j : i + 1, :],
+                    in1=metric_sb[a][:].unsqueeze(1).to_broadcast([P, i + 1 - j, D]),
+                    op=ALU.mult,
+                )
+                nc.sync.dma_start(
+                    out=out_0[a, r0 + j * P : r0 + (i + 1) * P, :].rearrange("(t p) f -> p t f", p=P),
+                    in_=y[s % 3][:, j : i + 1, :],
+                )
             elif kind == "H":
                 dst = yb[b][:, i, :].rearrange("p (u q e) -> p u q e", u=2, e=2)
                 src = y[s % 3][:, i, :].rearrange("p (q u e) -> p u q e", u=2, e=2)

@@ -14,24 +14,57 @@ U8 = mybir.dt.uint8
 FP8X4 = mybir.dt.float8_e4m3fn_x4
 FP4X4 = mybir.dt.float4_e2m1fn_x4
 ALU = mybir.AluOpType
-ACT = mybir.ActivationFunctionType
+FUNC = mybir.ActivationFunctionType
 
 P = 128
 STEP = 512
+HALF = STEP // 2
 STEPS = G * R // STEP
 TILES = STEP // P
+SCORE_TILES = J // P
+WORDS = D // 2
 RING = 7
 BIAS_ROW, RHO_ROW, PREC_ROW = 0, 8, 16
+EARLY_SCALE_STEPS = 5
 
-ORDER = "W M S D F X Ex S F Ex E E B G G S F B Ex D F B H B Qa G T J T Ex J Qa S Y T G T S Ex S W H I J S J Y R X M Ex M H S H Qx Ex Qy W E M E Ex I".split()
-COUNT = {"X": 2, "D": 2, "Qx": 1, "S": 8, "Ex": 8, "B": 4, "Qa": 2, "T": 4, "J": 4, "R": 1, "M": 4,
-         "E": 4, "F": 4, "G": 4, "H": 4, "Y": 2, "I": 2, "Qy": 1, "W": 3}
-PHASE = {"X":5,"D":4,"Qx":2,"S":7,"Ex":6,"B":0,"Qa":0,"T":0,"J":0,"R":0,"M":-1,"E":-2,"F":-4,"G":-4,"H":-4,"Y":-3,"I":-3,"Qy":-2,"W":3}
-CAST_ON = ["ACT","ACT","ACT","POOL"]
-WEIGH_ON = ["POOL","POOL","POOL","POOL"]
-WEIGH_WITH_NEXT = [0,0,0,0]
-TOT_PER_BANK = 1
-LEAD = 4
+CALLS = {
+    "X": 2,
+    "D": 2,
+    "Qx": 1,
+    "S": SCORE_TILES,
+    "Ex": SCORE_TILES,
+    "B": 4,
+    "Qa": 4,
+    "T": TILES,
+    "J": TILES,
+    "R": 1,
+    "M": TILES,
+    "E": TILES,
+    "F": TILES,
+    "G": TILES,
+    "H": TILES,
+    "Y": 2,
+    "I": 2,
+    "Qy": 2,
+    "W": 2 * G,
+    "WS": 1,
+    "K": 1,
+    "Mt": G,
+    "Mc": G,
+}
+
+HEAD = "W X W K X X Mt X Mt WS Mc D D Mt Mc W Qx S D S S W D Mt W Mc W Ex Ex X W Qx S D W Ex Mc S S S S Ex".split()
+LOOP = (
+    "Qa S H H S E J G Qa S Qa S Qy J M Qx H Ex M G Ex S F R B S Ex M E Ex Ex G S Ex E Ex H "
+    "Y E F G F Y X B D B Ex B I I X F T D T T T S Qy J Qa M J"
+).split()
+TAIL = (
+    "Y Qy Qa Qa Qa Qy I M Qa I I F Qy E G M M H E M E Qy F F E G I F Qy G F H H H G Y G H Y I I H Qy Y Qy Qy I Qy"
+).split()
+FIRST = {
+    "X": 2, "D": 2, "Qx": 0, "S": -4, "Ex": -5, "B": -4, "Qa": -7, "T": -4, "J": -6, "R": -2,
+    "M": -8, "E": -9, "F": -9, "G": -11, "H": -14, "Y": -9, "I": -9, "Qy": -11,
+}
 
 
 def tile_mean_shift_displacement_k7_kernel(
@@ -48,12 +81,11 @@ def tile_mean_shift_displacement_k7_kernel(
         def sbs(name, n, shape, dtype):
             return [sb("%s%d" % (name, k), shape, dtype) for k in range(n)]
 
-        banks = [psum.tile([P, 512], F32, name="bank%d" % k) for k in range(RING)]
-        const_bank = psum.tile([P, 4, P], BF16, name="const_bank")
+        banks = [psum.tile([P, STEP], F32, name="bank%d" % k) for k in range(RING)]
+        vector_bank = psum.tile([P, 4, P], BF16, name="vector_bank")
 
         ident = sb("ident", [P, P], F32)
         ident_bf = sb("ident_bf", [P, P], BF16)
-        warm = sb("warm", [P, 1], F32)
         rows = sb("rows", [P, 512], BF16)
         metric_rows = sb("metric_rows", [P, D], BF16)
         prec_sb = sb("prec_sb", [P, G, 4], BF16)
@@ -61,15 +93,15 @@ def tile_mean_shift_displacement_k7_kernel(
         metric_sb = sbs("metric_sb", G, [P, D], F32)
         x_sb = sbs("x_sb", STEPS, [P, TILES, D], BF16)
         b_raw = sbs("b_raw", G, [P, 2 * J], U8)
-        bs_raw = sb("bs_raw", [P, G, J], U8)
-        b_perm = sbs("b_perm", G, [P, 2 * J], U8)
-        bs_perm = sbs("bs_perm", G, [P, J], U8)
+        bs_raw = sb("bs_raw", [P, J], U8)
+        b_sorted = sbs("b_sorted", G, [P, 2 * J], U8)
+        bs_sorted = sbs("bs_sorted", G, [P, J], U8)
         h_sb = sbs("h_sb", G, [P, 2, 2 * D], U8)
         hs_sb = sb("hs_sb", [P, 2 * G, D], U8)
         xp = sbs("xp", 2, [P, STEP, 4], BF16)
         xq = sbs("xq", 2, [P, STEP], U32)
         xs = sbs("xs", 2, [P, STEP], U8)
-        aff = sbs("aff", 2, [P, 8, STEP], F32)
+        aff = sbs("aff", 2, [P, SCORE_TILES, STEP], F32)
         ar = sbs("ar", 2, [P, 2, STEP, 4], BF16)
         arq = sbs("arq", 2, [P, 2, STEP], U32)
         ars = sbs("ars", 2, [P, 2, STEP], U8)
@@ -102,58 +134,47 @@ def tile_mean_shift_displacement_k7_kernel(
                 in_=h_words[2 * a : 2 * a + 2].rearrange("g p n -> p g n").bitcast(I32),
             )
 
-        def load_scales(dst, src):
+        def load_b_scales():
             for q in range(4):
                 nc.sync.dma_start(
-                    out=dst[32 * q : 32 * q + 4, :, :].bitcast(I32),
-                    in_=src[:, 4 * q : 4 * q + 4, :].rearrange("g r n -> r g n").bitcast(I32),
+                    out=bs_raw[32 * q : 32 * q + 4 * G, :].bitcast(I32),
+                    in_=b_scales[:, 4 * q : 4 * q + 4, :].bitcast(I32),
+                )
+
+        def load_h_scales():
+            for q in range(4):
+                nc.sync.dma_start(
+                    out=hs_sb[32 * q : 32 * q + 4, :, :].bitcast(I32),
+                    in_=h_scales[:, 4 * q : 4 * q + 4, :].rearrange("g r n -> r g n").bitcast(I32),
                 )
 
         nc.vector.memset(rows[:].bitcast(I32), 0)
         nc.vector.memset(metric_rows[:].bitcast(I32), 0)
         nc.vector.memset(bs_raw[:].bitcast(I32), 0)
         nc.vector.memset(hs_sb[:].bitcast(I32), 0)
+        for a in range(1, G):
+            nc.vector.memset(bs_sorted[a][:].bitcast(I32), 0)
         make_identity(nc, ident_bf[:])
         make_identity(nc, ident[:])
         nc.scalar.dma_start(out=rows[PREC_ROW : PREC_ROW + G, :], in_=prec)
         nc.scalar.dma_start(out=rows[BIAS_ROW : BIAS_ROW + 2 * G, :], in_=bias.rearrange("a (g n) -> (a g) n", g=2))
         nc.scalar.dma_start(out=rows[RHO_ROW : RHO_ROW + 2 * G, :], in_=rho.rearrange("a (g n) -> (a g) n", g=2))
         nc.scalar.dma_start(out=metric_rows[0:G, :], in_=metric)
-        nc.scalar.activation(out=warm[:], in_=ident_bf[:, 0:1], func=ACT.Exp)
-        load_x(0, 0, 2)
+        load_x(0, 0, TILES // 2)
         load_b(0)
-        load_x(0, 2, 4)
-        load_scales(bs_raw, b_scales)
+        load_x(0, TILES // 2, TILES)
+        load_b_scales()
         load_x(1, 0, TILES)
         load_b(1)
-        load_h(0)
-        load_scales(hs_sb, h_scales)
         load_x(2, 0, TILES)
         load_b(2)
         load_b(3)
+        load_h(0)
+        load_h_scales()
         for s in range(3, STEPS):
             load_x(s, 0, TILES)
             if s % 2 == 1:
                 load_h(s // 2)
-
-        def permute(a, piece):
-            if piece < 2:
-                cols = slice(piece * J, (piece + 1) * J)
-                nc.vector.tensor_copy(
-                    out=b_perm[a][:, cols].rearrange("p (t m b) -> p t m b", t=4, b=2),
-                    in_=b_raw[a][:, cols].rearrange("p (m t b) -> p t m b", t=4, b=2),
-                )
-            else:
-                nc.vector.tensor_copy(
-                    out=bs_perm[a][:].rearrange("p (g t m) -> p g t m", g=2, t=4),
-                    in_=bs_raw[:, a, :].rearrange("p (g m t) -> p g t m", g=2, t=4),
-                )
-
-        for t in range(4):
-            nc.tensor.transpose(const_bank[:, t, :], rows[:, t : t + 4 * (P - 1) + 1 : 4], ident_bf[:])
-        nc.scalar.copy(prec_sb[:], const_bank[:, :, PREC_ROW : PREC_ROW + G].rearrange("p t a -> p a t"))
-        nc.scalar.copy(bias_sb[:], const_bank[:, :, BIAS_ROW : BIAS_ROW + 2 * G])
-        permute(0, 0)
 
         held = {}
 
@@ -161,106 +182,120 @@ def tile_mean_shift_displacement_k7_kernel(
             held[key] = banks[len(held) % RING]
             return held[key]
 
-        def turn_words(bank, words, first, step, half):
+        def turn_words(bank, words, half, u_offset, stride):
             for k in range(2):
                 for u in range(2):
-                    lo = (2 * half + k) * 256 + u * first
+                    lo = (2 * half + k) * WORDS + u * u_offset
                     nc.tensor.transpose(
-                        bank[:, u * 256 + k * P : u * 256 + (k + 1) * P],
-                        words[:, lo : lo + step * (P - 1) + 1 : step],
+                        bank[:, u * HALF + k * P : u * HALF + (k + 1) * P],
+                        words[:, lo : lo + stride * (P - 1) + 1 : stride],
                         ident[:],
                     )
 
-        def emit(kind, s, i):
+        def emit(code, s, i):
             a, r0, b = s // 2, (s % 2) * STEP, s % 2
-            if kind == "W":
-                if s + 1 < G:
-                    permute(s + 1, i)
-            elif kind == "X":
-                words = x_sb[s][:].rearrange("p t f -> p (t f)").bitcast(F32)
-                turn_words(take_bank(("X", s, i)), words, 1, 2, i)
-                if s == 0 and i == 1:
-                    for k in range(G):
-                        bank = take_bank(("metric", k))
-                        nc.tensor.matmul(
-                            bank[:],
-                            lhsT=ident_bf[:, k : k + 1].to_broadcast([P, P]),
-                            rhs=metric_rows[:],
-                            start=True,
-                            stop=True,
+            last = s == STEPS - 1
+            if code == "W":
+                cols = slice((i % 2) * J, (i % 2 + 1) * J)
+                nc.vector.tensor_copy(
+                    out=b_sorted[i // 2][:, cols].rearrange("p (t m b) -> p t m b", t=4, b=2),
+                    in_=b_raw[i // 2][:, cols].rearrange("p (m t b) -> p t m b", t=4, b=2),
+                )
+            elif code == "WS":
+                nc.vector.tensor_copy(
+                    out=bs_sorted[0][:].rearrange("p (g t m) -> p g t m", g=2, t=4),
+                    in_=bs_raw[:].rearrange("p (g m t) -> p g t m", g=2, t=4),
+                )
+                for group in range(1, G):
+                    for q in range(4):
+                        nc.sync.dma_start(
+                            out=bs_sorted[group][32 * q : 32 * q + 4, :].bitcast(I32),
+                            in_=bs_sorted[0][32 * q + 4 * group : 32 * q + 4 * group + 4, :].bitcast(I32),
                         )
-                        nc.scalar.copy(metric_sb[k][:], bank[:])
-            elif kind == "D":
+            elif code == "K":
+                for t in range(4):
+                    nc.tensor.transpose(vector_bank[:, t, :], rows[:, t : t + 4 * (P - 1) + 1 : 4], ident_bf[:])
+                nc.scalar.copy(prec_sb[:], vector_bank[:, :, PREC_ROW : PREC_ROW + G].rearrange("p t a -> p a t"))
+                nc.scalar.copy(bias_sb[:], vector_bank[:, :, BIAS_ROW : BIAS_ROW + 2 * G])
+            elif code == "Mt":
+                nc.tensor.matmul(
+                    take_bank(("Mt", s, i))[:],
+                    lhsT=ident_bf[:, i : i + 1].to_broadcast([P, P]),
+                    rhs=metric_rows[:],
+                    start=True,
+                    stop=True,
+                )
+            elif code == "Mc":
+                nc.scalar.copy(metric_sb[i][:], held["Mt", s, i][:])
+            elif code == "X":
+                words = x_sb[s][:].rearrange("p t f -> p (t f)").bitcast(F32)
+                turn_words(take_bank(("X", s, i)), words, i, 1, 2)
+            elif code == "D":
                 nc.vector.tensor_tensor(
-                    out=xp[b][:, i * 256 : (i + 1) * 256, :].rearrange("p n (u e) -> p n u e", u=2),
+                    out=xp[b][:, i * HALF : (i + 1) * HALF, :].rearrange("p n (u e) -> p n u e", u=2),
                     in0=held["X", s, i][:].bitcast(BF16).rearrange("p (u n e) -> p n u e", u=2, e=2),
-                    in1=prec_sb[:, a, :].rearrange("p (u e) -> p u e", u=2).unsqueeze(1).to_broadcast([P, 256, 2, 2]),
+                    in1=prec_sb[:, a, :].rearrange("p (u e) -> p u e", u=2).unsqueeze(1).to_broadcast([P, HALF, 2, 2]),
                     op=ALU.mult,
                 )
-                if s == 0 and i == 1:
-                    permute(0, 2)
-            elif kind == "Qx":
+            elif code == "Qx":
                 nc.vector.quantize_mx(
                     out=xq[b][:].bitcast(FP8X4), scales=xs[b][:], in_=xp[b][:].rearrange("p n t -> p (n t)")
                 )
-                if s == 0:
-                    permute(0, 1)
-            elif kind == "S":
+            elif code == "S":
                 nc.tensor.matmul_mx(
                     out=take_bank(("S", s, i))[:],
-                    lhsT=b_perm[a][:, i * 256 : (i + 1) * 256].bitcast(FP4X4),
-                    lhsT_scale=bs_perm[a][:, i * P : (i + 1) * P],
+                    lhsT=b_sorted[a][:, 2 * i * P : 2 * (i + 1) * P].bitcast(FP4X4),
+                    lhsT_scale=bs_sorted[a][:, i * P : (i + 1) * P],
                     rhs=xq[b][:].bitcast(FP8X4),
                     rhs_scale=xs[b][:],
                     start=True,
                     stop=True,
                 )
-            elif kind == "Ex":
+            elif code == "Ex":
+                g, t = divmod(i, 4)
                 nc.scalar.activation(
                     out=aff[b][:, i, :],
                     in_=held["S", s, i][:],
-                    func=ACT.Exp,
-                    bias=bias_sb[:, i % 4, 2 * a + i // 4 : 2 * a + i // 4 + 1],
+                    func=FUNC.Exp,
+                    bias=bias_sb[:, t, 2 * a + g : 2 * a + g + 1],
                 )
-            elif kind == "B":
-                g, n0 = i // 2, (i % 2) * 256
-                col = RHO_ROW + 2 * a + g
+            elif code == "B":
+                g, n0 = i // 2, (i % 2) * HALF
+                row = RHO_ROW + 2 * a + g
                 nc.vector.tensor_tensor(
-                    out=ar[b][:, g, n0 : n0 + 256, :].rearrange("p (c n) t -> p c t n", n=2),
-                    in0=aff[b][:, 4 * g : 4 * g + 4, n0 : n0 + 256].rearrange("p t (c n) -> p c t n", n=2),
-                    in1=const_bank[:, :, col : col + 1].unsqueeze(1).to_broadcast([P, 128, 4, 2]),
+                    out=ar[b][:, g, n0 : n0 + HALF, :].rearrange("p (c n) t -> p c t n", n=2),
+                    in0=aff[b][:, 4 * g : 4 * g + 4, n0 : n0 + HALF].rearrange("p t (c n) -> p c t n", n=2),
+                    in1=vector_bank[:, :, row : row + 1].unsqueeze(1).to_broadcast([P, HALF // 2, 4, 2]),
                     op=ALU.mult,
                 )
-            elif kind == "Qa":
+            elif code == "Qa":
+                g, half = i // 2, slice((i % 2) * HALF, (i % 2 + 1) * HALF)
                 nc.vector.quantize_mx(
-                    out=arq[b][:, i, :].bitcast(FP8X4),
-                    scales=ars[b][:, i, :],
-                    in_=ar[b][:, i, :, :].rearrange("p n t -> p (n t)"),
+                    out=arq[b][:, g, half].bitcast(FP8X4),
+                    scales=ars[b][:, g, half],
+                    in_=ar[b][:, g, half, :].rearrange("p n t -> p (n t)"),
                 )
-            elif kind == "T":
-                if i % TOT_PER_BANK == 0:
-                    take_bank(("T", s, i))
-                q = i % TOT_PER_BANK
-                for jt in range(8):
+            elif code == "T":
+                bank = take_bank(("T", s, i))
+                for jt in range(SCORE_TILES):
                     nc.tensor.matmul(
-                        held["T", s, i - q][:, q * P : (q + 1) * P],
+                        bank[:, 0:P],
                         lhsT=aff[b][:, jt, i * P : (i + 1) * P],
                         rhs=ident[:],
                         start=jt == 0,
-                        stop=jt == 7,
+                        stop=jt == SCORE_TILES - 1,
                         is_transpose=True,
                     )
-            elif kind == "J":
-                q = i % TOT_PER_BANK
+            elif code == "J":
                 nc.scalar.activation(
                     out=spill[:, i, :],
-                    in_=held["T", s, i - q][:, q * P : (q + 1) * P],
-                    func=ACT.Copy,
+                    in_=held["T", s, i][:, 0:P],
+                    func=FUNC.Copy,
                     accum_out=total[b][:, i : i + 1],
                 )
-            elif kind == "R":
+            elif code == "R":
                 nc.vector.reciprocal(rinv[b][:], total[b][:])
-            elif kind == "M":
+            elif code == "M":
                 bank = take_bank(("M", s, i))
                 for g in range(2):
                     nc.tensor.matmul_mx(
@@ -272,7 +307,7 @@ def tile_mean_shift_displacement_k7_kernel(
                         start=g == 0,
                         stop=g == 1,
                     )
-            elif kind == "E":
+            elif code == "E":
                 nc.vector.scalar_tensor_tensor(
                     out=disp[b][:, i, :],
                     in0=held["M", s, i][:],
@@ -281,66 +316,76 @@ def tile_mean_shift_displacement_k7_kernel(
                     op0=ALU.mult,
                     op1=ALU.subtract,
                 )
-            elif kind == "F":
-                nc.scalar.activation(out=sq[b][:, i, :], in_=disp[b][:, i, :], func=ACT.Square)
-            elif kind == "G":
-                last = s == STEPS - 1
-                if WEIGH_WITH_NEXT[i] and not last:
-                    return
-                j = i
-                while j > 0 and WEIGH_WITH_NEXT[j - 1] and not last:
-                    j -= 1
-                eng = nc.vector if last or WEIGH_ON[i] == "DVE" else nc.gpsimd
-                eng.tensor_tensor(
-                    out=y[s % 3][:, j : i + 1, :],
-                    in0=sq[b][:, j : i + 1, :],
-                    in1=metric_sb[a][:].unsqueeze(1).to_broadcast([P, i + 1 - j, D]),
-                    op=ALU.mult,
-                )
-                nc.sync.dma_start(
-                    out=out_0[a, r0 + j * P : r0 + (i + 1) * P, :].rearrange("(t p) f -> p t f", p=P),
-                    in_=y[s % 3][:, j : i + 1, :],
-                )
-            elif kind == "H":
+            elif code == "F":
+                nc.scalar.activation(out=sq[b][:, i, :], in_=disp[b][:, i, :], func=FUNC.Square)
+            elif code == "G":
+                if last or i % 2 == 1:
+                    t0 = i if last else i - 1
+                    engine = nc.vector if last else nc.gpsimd
+                    engine.tensor_tensor(
+                        out=y[s % 3][:, t0 : i + 1, :],
+                        in0=sq[b][:, t0 : i + 1, :],
+                        in1=metric_sb[a][:].unsqueeze(1).to_broadcast([P, i + 1 - t0, D]),
+                        op=ALU.mult,
+                    )
+                    nc.sync.dma_start(
+                        out=out_0[a, r0 + t0 * P : r0 + (i + 1) * P, :].rearrange("(t p) f -> p t f", p=P),
+                        in_=y[s % 3][:, t0 : i + 1, :],
+                    )
+            elif code == "H":
                 dst = yb[b][:, i, :].rearrange("p (u q e) -> p u q e", u=2, e=2)
                 src = y[s % 3][:, i, :].rearrange("p (q u e) -> p u q e", u=2, e=2)
-                where = CAST_ON[i] if s < STEPS - 1 else ("ACT", "DVE")[i % 2]
-                if where == "ACT":
+                if i in ((0, 1) if last else (0, 3)):
                     nc.scalar.copy(dst, src)
-                elif where == "DVE":
+                elif last:
                     nc.vector.tensor_copy(dst, src)
                 else:
                     nc.gpsimd.tensor_scalar(dst, src, 1.0, 1.0, ALU.mult, ALU.mult)
-            elif kind == "Y":
+            elif code == "Y":
                 words = yb[b][:].rearrange("p t f -> p (t f)").bitcast(F32)
-                turn_words(take_bank(("Y", s, i)), words, P, 1, i)
-            elif kind == "I":
+                turn_words(take_bank(("Y", s, i)), words, i, P, 1)
+            elif code == "I":
                 words = yt[b][:].rearrange("p n t -> p (n t)").bitcast(F32)
                 nc.scalar.copy(
-                    words[:, i * 512 : (i + 1) * 512].rearrange("p (n u) -> p n u", u=2),
+                    words[:, 2 * i * HALF : 2 * (i + 1) * HALF].rearrange("p (n u) -> p n u", u=2),
                     held["Y", s, i][:].rearrange("p (u n) -> p n u", u=2),
                 )
-            elif kind == "Qy":
-                cols = slice(s * STEP, (s + 1) * STEP)
+            elif code == "Qy":
+                half = slice(i * HALF, (i + 1) * HALF)
+                cols = slice(s * STEP + i * HALF, s * STEP + (i + 1) * HALF)
                 nc.vector.quantize_mx(
-                    out=yq[b][:].bitcast(FP8X4), scales=ys[:, cols], in_=yt[b][:].rearrange("p n t -> p (n t)")
+                    out=yq[b][:, half].bitcast(FP8X4),
+                    scales=ys[:, cols],
+                    in_=yt[b][:, half, :].rearrange("p n t -> p (n t)"),
                 )
                 nc.sync.dma_start(
-                    out=out_1[0, :, cols, :].rearrange("p n t -> p (n t)").bitcast(I32), in_=yq[b][:].bitcast(I32)
+                    out=out_1[0, :, cols, :].rearrange("p n t -> p (n t)").bitcast(I32),
+                    in_=yq[b][:, half].bitcast(I32),
                 )
-                if s >= STEPS - 2:
-                    done = slice(0, (STEPS - 1) * STEP) if s == STEPS - 2 else cols
+                if i == 1 and (last or s == EARLY_SCALE_STEPS - 1):
+                    done = slice(EARLY_SCALE_STEPS * STEP if last else 0, (s + 1) * STEP)
                     for q in range(4):
-                        queue = nc.scalar if s == STEPS - 1 and q % 2 else nc.sync
+                        queue = nc.scalar if last and q % 2 else nc.sync
                         queue.dma_start(
                             out=out_2[0, 4 * q : 4 * q + 4, done].bitcast(I32),
                             in_=ys[32 * q : 32 * q + 4, done].bitcast(I32),
                         )
 
-        seen = {kind: PHASE[kind] - LEAD * COUNT[kind] for kind in COUNT}
-        for turn in range(STEPS + 2 * LEAD + 1):
-            for kind in ORDER:
-                s, i = divmod(seen[kind], COUNT[kind])
-                seen[kind] += 1
-                if 0 <= s < STEPS:
-                    emit(kind, s, i)
+        made = {code: 0 for code in CALLS}
+
+        def emit_next(code):
+            s, i = divmod(made[code], CALLS[code])
+            made[code] += 1
+            emit(code, s, i)
+
+        for code in HEAD:
+            emit_next(code)
+        due = dict(FIRST)
+        loop_end = {code: STEPS * CALLS[code] - len([c for c in TAIL if c == code]) for code in FIRST}
+        while any(made[code] < loop_end[code] for code in FIRST):
+            for code in LOOP:
+                if made[code] == due[code] < loop_end[code]:
+                    emit_next(code)
+                due[code] += 1
+        for code in TAIL:
+            emit_next(code)

from contextlib import ExitStack

import concourse.mybir as mybir
from concourse.masks import make_identity

G, R, D, J = 4, 1024, 512, 1024
FLOPS = 2 * 2 * G * R * D * J

F32 = mybir.dt.float32
BF16 = mybir.dt.bfloat16
I32 = mybir.dt.int32
U32 = mybir.dt.uint32
U8 = mybir.dt.uint8
FP8X4 = mybir.dt.float8_e4m3fn_x4
FP4X4 = mybir.dt.float4_e2m1fn_x4
ALU = mybir.AluOpType
FUNC = mybir.ActivationFunctionType

P = 128
STEP = 512
HALF = STEP // 2
STEPS = G * R // STEP
TILES = STEP // P
SCORE_TILES = J // P
WORDS = D // 2
RING = 7
BIAS_ROW, RHO_ROW, PREC_ROW = 0, 8, 16
EARLY_SCALE_STEPS = 5

CALLS = {
    "X": 2,
    "D": 2,
    "Qx": 1,
    "S": SCORE_TILES,
    "Ex": SCORE_TILES,
    "B": 4,
    "Qa": 4,
    "T": TILES,
    "J": TILES,
    "R": 1,
    "M": TILES,
    "E": TILES,
    "F": TILES,
    "G": TILES,
    "H": TILES,
    "Y": 2,
    "I": 2,
    "Qy": 2,
    "W": 2 * G,
    "WS": 1,
    "K": 1,
    "Mt": G,
    "Mc": G,
}

HEAD = "W X W K X X Mt X Mt WS Mc D D Mt Mc W Qx S D S S W D Mt W Mc W Ex Ex X W Qx S D W Ex Mc S S S S Ex".split()
LOOP = (
    "Qa S H H S E J G Qa S Qa S Qy J M Qx H Ex M G Ex S F R B S Ex M E Ex Ex G S Ex E Ex H "
    "Y E F G F Y X B D B Ex B I I X F T D T T T S Qy J Qa M J"
).split()
TAIL = (
    "Y Qy Qa Qa Qa Qy I M Qa I I F Qy E G M M H E M E Qy F F E G I F Qy G F H H H G Y G H Y I I H Qy Y Qy Qy I Qy"
).split()
FIRST = {
    "X": 2, "D": 2, "Qx": 0, "S": -4, "Ex": -5, "B": -4, "Qa": -7, "T": -4, "J": -6, "R": -2,
    "M": -8, "E": -9, "F": -9, "G": -11, "H": -14, "Y": -9, "I": -9, "Qy": -11,
}


def tile_mean_shift_displacement_k7_kernel(
    tc, x, prec, b_words, b_scales, bias, rho, h_words, h_scales, metric, out_0, out_1, out_2
):
    nc = tc.nc
    with ExitStack() as ctx:
        keep = ctx.enter_context(tc.tile_pool(name="keep", bufs=1))
        psum = ctx.enter_context(tc.psum_pool(name="psum", bufs=1))

        def sb(name, shape, dtype):
            return keep.tile(shape, dtype, name=name, align_bytes=64)

        def sbs(name, n, shape, dtype):
            return [sb("%s%d" % (name, k), shape, dtype) for k in range(n)]

        banks = [psum.tile([P, STEP], F32, name="bank%d" % k) for k in range(RING)]
        vector_bank = psum.tile([P, 4, P], BF16, name="vector_bank")

        ident = sb("ident", [P, P], F32)
        ident_bf = sb("ident_bf", [P, P], BF16)
        rows = sb("rows", [P, 512], BF16)
        metric_rows = sb("metric_rows", [P, D], BF16)
        prec_sb = sb("prec_sb", [P, G, 4], BF16)
        bias_sb = sb("bias_sb", [P, 4, 2 * G], F32)
        metric_sb = sbs("metric_sb", G, [P, D], F32)
        x_sb = sbs("x_sb", STEPS, [P, TILES, D], BF16)
        b_raw = sbs("b_raw", G, [P, 2 * J], U8)
        bs_raw = sb("bs_raw", [P, J], U8)
        b_sorted = sbs("b_sorted", G, [P, 2 * J], U8)
        bs_sorted = sbs("bs_sorted", G, [P, J], U8)
        h_sb = sbs("h_sb", G, [P, 2, 2 * D], U8)
        hs_sb = sb("hs_sb", [P, 2 * G, D], U8)
        xp = sbs("xp", 2, [P, STEP, 4], BF16)
        xq = sbs("xq", 2, [P, STEP], U32)
        xs = sbs("xs", 2, [P, STEP], U8)
        aff = sbs("aff", 2, [P, SCORE_TILES, STEP], F32)
        ar = sbs("ar", 2, [P, 2, STEP, 4], BF16)
        arq = sbs("arq", 2, [P, 2, STEP], U32)
        ars = sbs("ars", 2, [P, 2, STEP], U8)
        spill = sb("spill", [P, TILES, P], BF16)
        total = sbs("total", 2, [P, TILES], F32)
        rinv = sbs("rinv", 2, [P, TILES], F32)
        disp = sbs("disp", 2, [P, TILES, D], F32)
        sq = sbs("sq", 2, [P, TILES, D], F32)
        y = sbs("y", 3, [P, TILES, D], F32)
        yb = sbs("yb", 2, [P, TILES, D], BF16)
        yt = sbs("yt", 2, [P, STEP, 4], BF16)
        yq = sbs("yq", 2, [P, STEP], U32)
        ys = sb("ys", [P, G * R], U8)

        ctx.enter_context(tc.manual_schedule())

        def load_x(s, t0, t1):
            a, r0 = s // 2, (s % 2) * STEP
            nc.sync.dma_start(
                out=x_sb[s][:, t0:t1, :],
                in_=x[a, r0 + t0 * P : r0 + t1 * P, :].rearrange("(t p) f -> p t f", p=P),
            )

        def load_b(a):
            nc.sync.dma_start(out=b_raw[a][:].bitcast(I32), in_=b_words[a].bitcast(I32))

        def load_h(a):
            nc.sync.dma_start(
                out=h_sb[a][:].bitcast(I32),
                in_=h_words[2 * a : 2 * a + 2].rearrange("g p n -> p g n").bitcast(I32),
            )

        def load_b_scales():
            for q in range(4):
                nc.sync.dma_start(
                    out=bs_raw[32 * q : 32 * q + 4 * G, :].bitcast(I32),
                    in_=b_scales[:, 4 * q : 4 * q + 4, :].bitcast(I32),
                )

        def load_h_scales():
            for q in range(4):
                nc.sync.dma_start(
                    out=hs_sb[32 * q : 32 * q + 4, :, :].bitcast(I32),
                    in_=h_scales[:, 4 * q : 4 * q + 4, :].rearrange("g r n -> r g n").bitcast(I32),
                )

        nc.vector.memset(rows[:].bitcast(I32), 0)
        nc.vector.memset(metric_rows[:].bitcast(I32), 0)
        nc.vector.memset(bs_raw[:].bitcast(I32), 0)
        nc.vector.memset(hs_sb[:].bitcast(I32), 0)
        for a in range(1, G):
            nc.vector.memset(bs_sorted[a][:].bitcast(I32), 0)
        make_identity(nc, ident_bf[:])
        make_identity(nc, ident[:])
        nc.scalar.dma_start(out=rows[PREC_ROW : PREC_ROW + G, :], in_=prec)
        nc.scalar.dma_start(out=rows[BIAS_ROW : BIAS_ROW + 2 * G, :], in_=bias.rearrange("a (g n) -> (a g) n", g=2))
        nc.scalar.dma_start(out=rows[RHO_ROW : RHO_ROW + 2 * G, :], in_=rho.rearrange("a (g n) -> (a g) n", g=2))
        nc.scalar.dma_start(out=metric_rows[0:G, :], in_=metric)
        load_x(0, 0, TILES // 2)
        load_b(0)
        load_x(0, TILES // 2, TILES)
        load_b_scales()
        load_x(1, 0, TILES)
        load_b(1)
        load_x(2, 0, TILES)
        load_b(2)
        load_b(3)
        load_h(0)
        load_h_scales()
        for s in range(3, STEPS):
            load_x(s, 0, TILES)
            if s % 2 == 1:
                load_h(s // 2)

        held = {}

        def take_bank(key):
            held[key] = banks[len(held) % RING]
            return held[key]

        def turn_words(bank, words, half, u_offset, stride):
            for k in range(2):
                for u in range(2):
                    lo = (2 * half + k) * WORDS + u * u_offset
                    nc.tensor.transpose(
                        bank[:, u * HALF + k * P : u * HALF + (k + 1) * P],
                        words[:, lo : lo + stride * (P - 1) + 1 : stride],
                        ident[:],
                    )

        def emit(code, s, i):
            a, r0, b = s // 2, (s % 2) * STEP, s % 2
            last = s == STEPS - 1
            if code == "W":
                cols = slice((i % 2) * J, (i % 2 + 1) * J)
                nc.vector.tensor_copy(
                    out=b_sorted[i // 2][:, cols].rearrange("p (t m b) -> p t m b", t=4, b=2),
                    in_=b_raw[i // 2][:, cols].rearrange("p (m t b) -> p t m b", t=4, b=2),
                )
            elif code == "WS":
                nc.vector.tensor_copy(
                    out=bs_sorted[0][:].rearrange("p (g t m) -> p g t m", g=2, t=4),
                    in_=bs_raw[:].rearrange("p (g m t) -> p g t m", g=2, t=4),
                )
                for group in range(1, G):
                    for q in range(4):
                        nc.sync.dma_start(
                            out=bs_sorted[group][32 * q : 32 * q + 4, :].bitcast(I32),
                            in_=bs_sorted[0][32 * q + 4 * group : 32 * q + 4 * group + 4, :].bitcast(I32),
                        )
            elif code == "K":
                for t in range(4):
                    nc.tensor.transpose(vector_bank[:, t, :], rows[:, t : t + 4 * (P - 1) + 1 : 4], ident_bf[:])
                nc.scalar.copy(prec_sb[:], vector_bank[:, :, PREC_ROW : PREC_ROW + G].rearrange("p t a -> p a t"))
                nc.scalar.copy(bias_sb[:], vector_bank[:, :, BIAS_ROW : BIAS_ROW + 2 * G])
            elif code == "Mt":
                nc.tensor.matmul(
                    take_bank(("Mt", s, i))[:],
                    lhsT=ident_bf[:, i : i + 1].to_broadcast([P, P]),
                    rhs=metric_rows[:],
                    start=True,
                    stop=True,
                )
            elif code == "Mc":
                nc.scalar.copy(metric_sb[i][:], held["Mt", s, i][:])
            elif code == "X":
                words = x_sb[s][:].rearrange("p t f -> p (t f)").bitcast(F32)
                turn_words(take_bank(("X", s, i)), words, i, 1, 2)
            elif code == "D":
                nc.vector.tensor_tensor(
                    out=xp[b][:, i * HALF : (i + 1) * HALF, :].rearrange("p n (u e) -> p n u e", u=2),
                    in0=held["X", s, i][:].bitcast(BF16).rearrange("p (u n e) -> p n u e", u=2, e=2),
                    in1=prec_sb[:, a, :].rearrange("p (u e) -> p u e", u=2).unsqueeze(1).to_broadcast([P, HALF, 2, 2]),
                    op=ALU.mult,
                )
            elif code == "Qx":
                nc.vector.quantize_mx(
                    out=xq[b][:].bitcast(FP8X4), scales=xs[b][:], in_=xp[b][:].rearrange("p n t -> p (n t)")
                )
            elif code == "S":
                nc.tensor.matmul_mx(
                    out=take_bank(("S", s, i))[:],
                    lhsT=b_sorted[a][:, 2 * i * P : 2 * (i + 1) * P].bitcast(FP4X4),
                    lhsT_scale=bs_sorted[a][:, i * P : (i + 1) * P],
                    rhs=xq[b][:].bitcast(FP8X4),
                    rhs_scale=xs[b][:],
                    start=True,
                    stop=True,
                )
            elif code == "Ex":
                g, t = divmod(i, 4)
                nc.scalar.activation(
                    out=aff[b][:, i, :],
                    in_=held["S", s, i][:],
                    func=FUNC.Exp,
                    bias=bias_sb[:, t, 2 * a + g : 2 * a + g + 1],
                )
            elif code == "B":
                g, n0 = i // 2, (i % 2) * HALF
                row = RHO_ROW + 2 * a + g
                nc.vector.tensor_tensor(
                    out=ar[b][:, g, n0 : n0 + HALF, :].rearrange("p (c n) t -> p c t n", n=2),
                    in0=aff[b][:, 4 * g : 4 * g + 4, n0 : n0 + HALF].rearrange("p t (c n) -> p c t n", n=2),
                    in1=vector_bank[:, :, row : row + 1].unsqueeze(1).to_broadcast([P, HALF // 2, 4, 2]),
                    op=ALU.mult,
                )
            elif code == "Qa":
                g, half = i // 2, slice((i % 2) * HALF, (i % 2 + 1) * HALF)
                nc.vector.quantize_mx(
                    out=arq[b][:, g, half].bitcast(FP8X4),
                    scales=ars[b][:, g, half],
                    in_=ar[b][:, g, half, :].rearrange("p n t -> p (n t)"),
                )
            elif code == "T":
                bank = take_bank(("T", s, i))
                for jt in range(SCORE_TILES):
                    nc.tensor.matmul(
                        bank[:, 0:P],
                        lhsT=aff[b][:, jt, i * P : (i + 1) * P],
                        rhs=ident[:],
                        start=jt == 0,
                        stop=jt == SCORE_TILES - 1,
                        is_transpose=True,
                    )
            elif code == "J":
                nc.scalar.activation(
                    out=spill[:, i, :],
                    in_=held["T", s, i][:, 0:P],
                    func=FUNC.Copy,
                    accum_out=total[b][:, i : i + 1],
                )
            elif code == "R":
                nc.vector.reciprocal(rinv[b][:], total[b][:])
            elif code == "M":
                bank = take_bank(("M", s, i))
                for g in range(2):
                    nc.tensor.matmul_mx(
                        out=bank[:],
                        lhsT=arq[b][:, g, i * P : (i + 1) * P].bitcast(FP8X4),
                        lhsT_scale=ars[b][:, g, i * P : (i + 1) * P],
                        rhs=h_sb[a][:, g, :].bitcast(FP4X4),
                        rhs_scale=hs_sb[:, 2 * a + g, :],
                        start=g == 0,
                        stop=g == 1,
                    )
            elif code == "E":
                nc.vector.scalar_tensor_tensor(
                    out=disp[b][:, i, :],
                    in0=held["M", s, i][:],
                    scalar=rinv[b][:, i : i + 1],
                    in1=x_sb[s][:, i, :],
                    op0=ALU.mult,
                    op1=ALU.subtract,
                )
            elif code == "F":
                nc.scalar.activation(out=sq[b][:, i, :], in_=disp[b][:, i, :], func=FUNC.Square)
            elif code == "G":
                if last or i % 2 == 1:
                    t0 = i if last else i - 1
                    engine = nc.vector if last else nc.gpsimd
                    engine.tensor_tensor(
                        out=y[s % 3][:, t0 : i + 1, :],
                        in0=sq[b][:, t0 : i + 1, :],
                        in1=metric_sb[a][:].unsqueeze(1).to_broadcast([P, i + 1 - t0, D]),
                        op=ALU.mult,
                    )
                    nc.sync.dma_start(
                        out=out_0[a, r0 + t0 * P : r0 + (i + 1) * P, :].rearrange("(t p) f -> p t f", p=P),
                        in_=y[s % 3][:, t0 : i + 1, :],
                    )
            elif code == "H":
                dst = yb[b][:, i, :].rearrange("p (u q e) -> p u q e", u=2, e=2)
                src = y[s % 3][:, i, :].rearrange("p (q u e) -> p u q e", u=2, e=2)
                if i in ((0, 1) if last else (0, 3)):
                    nc.scalar.copy(dst, src)
                elif last:
                    nc.vector.tensor_copy(dst, src)
                else:
                    nc.gpsimd.tensor_scalar(dst, src, 1.0, 1.0, ALU.mult, ALU.mult)
            elif code == "Y":
                words = yb[b][:].rearrange("p t f -> p (t f)").bitcast(F32)
                turn_words(take_bank(("Y", s, i)), words, i, P, 1)
            elif code == "I":
                words = yt[b][:].rearrange("p n t -> p (n t)").bitcast(F32)
                nc.scalar.copy(
                    words[:, 2 * i * HALF : 2 * (i + 1) * HALF].rearrange("p (n u) -> p n u", u=2),
                    held["Y", s, i][:].rearrange("p (u n) -> p n u", u=2),
                )
            elif code == "Qy":
                half = slice(i * HALF, (i + 1) * HALF)
                cols = slice(s * STEP + i * HALF, s * STEP + (i + 1) * HALF)
                nc.vector.quantize_mx(
                    out=yq[b][:, half].bitcast(FP8X4),
                    scales=ys[:, cols],
                    in_=yt[b][:, half, :].rearrange("p n t -> p (n t)"),
                )
                nc.sync.dma_start(
                    out=out_1[0, :, cols, :].rearrange("p n t -> p (n t)").bitcast(I32),
                    in_=yq[b][:, half].bitcast(I32),
                )
                if i == 1 and (last or s == EARLY_SCALE_STEPS - 1):
                    done = slice(EARLY_SCALE_STEPS * STEP if last else 0, (s + 1) * STEP)
                    for q in range(4):
                        queue = nc.scalar if last and q % 2 else nc.sync
                        queue.dma_start(
                            out=out_2[0, 4 * q : 4 * q + 4, done].bitcast(I32),
                            in_=ys[32 * q : 32 * q + 4, done].bitcast(I32),
                        )

        made = {code: 0 for code in CALLS}

        def emit_next(code):
            s, i = divmod(made[code], CALLS[code])
            made[code] += 1
            emit(code, s, i)

        for code in HEAD:
            emit_next(code)
        due = dict(FIRST)
        loop_end = {code: STEPS * CALLS[code] - len([c for c in TAIL if c == code]) for code in FIRST}
        while any(made[code] < loop_end[code] for code in FIRST):
            for code in LOOP:
                if made[code] == due[code] < loop_end[code]:
                    emit_next(code)
                due[code] += 1
        for code in TAIL:
            emit_next(code)
